import numpy as np
import ml_dtypes

BF16 = ml_dtypes.bfloat16


def bf(x):
    return np.asarray(x, np.float32).astype(BF16)


def f32(x):
    return np.asarray(x, np.float32)


def f64(x):
    return np.asarray(x).astype(np.float64)


def striped(idx):
    return np.concatenate([l.reshape(-1, 16).T for l in idx])


def rows(idx, k):
    return np.tile(np.repeat(idx, 16, axis=0), (k // (16 * 8), 1))


def look(tab, idx):
    return np.take_along_axis(f64(tab), rows(idx, len(tab)), axis=1)


K, S, V, N, M = 256, 2048, 2048, 2048, 128


def silu(v):
    return v / (1.0 + np.exp(-v))


def setup_inputs():
    return {"tab": f32(np.random.standard_normal((2, K, S))), "y": f32(np.random.standard_normal((K, V))), "w": bf(np.random.standard_normal((K, M)) / np.sqrt(K)), "b": f32(0.5 * np.random.standard_normal((M, 1))), "offs": striped(np.stack([np.random.permutation(S)[:N] for _ in range(8)]))}


def reference(tab, y, w, b, offs):
    idx = np.stack([g.T.reshape(-1) for g in np.split(offs, 8)])
    x = (look(tab[0], idx) * f64(y)) * (silu(look(tab[1], idx)))
    return np.maximum(f64(w).T @ x + f64(b), 0.0)

@@ -1,0 +1,52 @@
+import concourse.mybir as mybir
+
+F32, BF16, U16 = mybir.dt.float32, mybir.dt.bfloat16, mybir.dt.uint16
+MULT = mybir.AluOpType.mult
+SILU, RELU = mybir.ActivationFunctionType.Silu, mybir.ActivationFunctionType.Relu
+
+P = 128
+K, S, N, M = 256, 2048, 2048, 128
+PIECE = 512
+GROUP = 16
+BLOCKS, PIECES = K // P, N // PIECE
+
+FLOPS = 2 * K * M * N
+
+
+def tile_lookup_vg_mulsilu_relu_kernel(tc, tab, y, w, b, offs, out):
+    nc = tc.nc
+    with (
+        tc.tile_pool(name="held", bufs=1) as held,
+        tc.psum_pool(name="psum", bufs=1) as psum,
+    ):
+        offsets = held.tile([P, N // GROUP], U16, name="offsets")
+        weights = held.tile([P, BLOCKS, M], BF16, name="weights")
+        bias = held.tile([M, 1], F32, name="bias")
+        banks = [psum.tile([M, PIECE], F32, name=f"bank{j}") for j in range(PIECES)]
+
+        nc.sync.dma_start(offsets[:], offs)
+        nc.scalar.dma_start(weights[:], w.rearrange("(k p) m -> p k m", p=P))
+        nc.scalar.dma_start(bias[:], b)
+
+        for k in range(BLOCKS):
+            rows = slice(k * P, (k + 1) * P)
+            values = held.tile([P, S], F32, name=f"values{k}")
+            gates = held.tile([P, S], F32, name=f"gates{k}")
+            nc.sync.dma_start(values[:], tab[0, rows, :])
+            nc.sync.dma_start(gates[:], tab[1, rows, :])
+            for j in range(PIECES):
+                cols = slice(j * PIECE, (j + 1) * PIECE)
+                entries = offsets[:, j * PIECE // GROUP : (j + 1) * PIECE // GROUP]
+                stream = held.tile([P, PIECE], F32, name=f"stream{k}_{j}")
+                scaled = held.tile([P, PIECE], F32, name=f"scaled{k}_{j}")
+                gated = held.tile([P, PIECE], F32, name=f"gated{k}_{j}")
+                x = held.tile([P, PIECE], BF16, name=f"x{k}_{j}")
+                nc.sync.dma_start(stream[:], y[rows, cols])
+                nc.vector.tensor_tensor(scaled[:], values[:].indirect(entries), stream[:], MULT)
+                nc.scalar.activation(gated[:], gates[:].indirect(entries), SILU)
+                nc.vector.tensor_tensor(x[:], scaled[:], gated[:], MULT)
+                nc.tensor.matmul(banks[j][:], weights[:, k, :], x[:], start=k == 0, stop=k == BLOCKS - 1)
+                if k == BLOCKS - 1:
+                    result = held.tile([M, PIECE], F32, name=f"result{j}")
+                    nc.scalar.activation(result[:], banks[j][:], RELU, bias=bias[:])
+                    nc.sync.dma_start(out[:, cols], result[:])

@@ -1,7 +1,7 @@
 import concourse.mybir as mybir
 
 F32, BF16, U16 = mybir.dt.float32, mybir.dt.bfloat16, mybir.dt.uint16
-MULT = mybir.AluOpType.mult
+MULT, ADD, MAX = mybir.AluOpType.mult, mybir.AluOpType.add, mybir.AluOpType.max
 SILU, RELU = mybir.ActivationFunctionType.Silu, mybir.ActivationFunctionType.Relu
 
 P = 128
@@ -28,25 +28,36 @@ def tile_lookup_vg_mulsilu_relu_kernel(tc, tab, y, w, b, offs, out):
         nc.scalar.dma_start(weights[:], w.rearrange("(k p) m -> p k m", p=P))
         nc.scalar.dma_start(bias[:], b)
 
+        scratch = held.tile([P, 1], F32, name="scratch")
+        warmed = held.tile([P, 1], F32, name="warmed")
+        nc.vector.memset(scratch[:], 0.0)
+        nc.scalar.activation(warmed[:], scratch[:], SILU)
+
         for k in range(BLOCKS):
             rows = slice(k * P, (k + 1) * P)
             values = held.tile([P, S], F32, name=f"values{k}")
             gates = held.tile([P, S], F32, name=f"gates{k}")
+            streams = [held.tile([P, PIECE], F32, name=f"stream{k}_{j}") for j in range(PIECES)]
             nc.sync.dma_start(values[:], tab[0, rows, :])
-            nc.sync.dma_start(gates[:], tab[1, rows, :])
             for j in range(PIECES):
-                cols = slice(j * PIECE, (j + 1) * PIECE)
+                if j == PIECES // 2:
+                    nc.sync.dma_start(gates[:], tab[1, rows, :])
+                nc.sync.dma_start(streams[j][:], y[rows, j * PIECE : (j + 1) * PIECE])
+
+            for j in range(PIECES):
                 entries = offsets[:, j * PIECE // GROUP : (j + 1) * PIECE // GROUP]
-                stream = held.tile([P, PIECE], F32, name=f"stream{k}_{j}")
                 scaled = held.tile([P, PIECE], F32, name=f"scaled{k}_{j}")
                 gated = held.tile([P, PIECE], F32, name=f"gated{k}_{j}")
                 x = held.tile([P, PIECE], BF16, name=f"x{k}_{j}")
-                nc.sync.dma_start(stream[:], y[rows, cols])
-                nc.vector.tensor_tensor(scaled[:], values[:].indirect(entries), stream[:], MULT)
+                nc.vector.tensor_tensor(scaled[:], values[:].indirect(entries), streams[j][:], MULT)
                 nc.scalar.activation(gated[:], gates[:].indirect(entries), SILU)
                 nc.vector.tensor_tensor(x[:], scaled[:], gated[:], MULT)
                 nc.tensor.matmul(banks[j][:], weights[:, k, :], x[:], start=k == 0, stop=k == BLOCKS - 1)
-                if k == BLOCKS - 1:
-                    result = held.tile([M, PIECE], F32, name=f"result{j}")
-                    nc.scalar.activation(result[:], banks[j][:], RELU, bias=bias[:])
-                    nc.sync.dma_start(out[:, cols], result[:])
+
+        for j in range(PIECES):
+            result = held.tile([M, PIECE], F32, name=f"result{j}")
+            if j % 2 == 0:
+                nc.scalar.activation(result[:], banks[j][:], RELU, bias=bias[:])
+            else:
+                nc.vector.tensor_scalar(result[:], banks[j][:], bias[:], 0.0, ADD, MAX)
+            nc.sync.dma_start(out[:, j * PIECE : (j + 1) * PIECE], result[:])

@@ -10,6 +10,8 @@ PIECE = 512
 GROUP = 16
 BLOCKS, PIECES = K // P, N // PIECE
 
+LAG = PIECES // 2
+
 FLOPS = 2 * K * M * N
 
 
@@ -22,42 +24,66 @@ def tile_lookup_vg_mulsilu_relu_kernel(tc, tab, y, w, b, offs, out):
         offsets = held.tile([P, N // GROUP], U16, name="offsets")
         weights = held.tile([P, BLOCKS, M], BF16, name="weights")
         bias = held.tile([M, 1], F32, name="bias")
-        banks = [psum.tile([M, PIECE], F32, name=f"bank{j}") for j in range(PIECES)]
+        parts = {j: 2 if j >= PIECES - LAG else 1 for j in range(PIECES)}
+        banks = {
+            (j, h): psum.tile([M, PIECE // parts[j]], F32, name=f"bank{j}_{h}")
+            for j in range(PIECES)
+            for h in range(parts[j])
+        }
 
         nc.sync.dma_start(offsets[:], offs)
-        nc.scalar.dma_start(weights[:], w.rearrange("(k p) m -> p k m", p=P))
-        nc.scalar.dma_start(bias[:], b)
 
         scratch = held.tile([P, 1], F32, name="scratch")
         warmed = held.tile([P, 1], F32, name="warmed")
         nc.vector.memset(scratch[:], 0.0)
         nc.scalar.activation(warmed[:], scratch[:], SILU)
 
+        values, gates, streams = {}, {}, {}
         for k in range(BLOCKS):
             rows = slice(k * P, (k + 1) * P)
-            values = held.tile([P, S], F32, name=f"values{k}")
-            gates = held.tile([P, S], F32, name=f"gates{k}")
-            streams = [held.tile([P, PIECE], F32, name=f"stream{k}_{j}") for j in range(PIECES)]
-            nc.sync.dma_start(values[:], tab[0, rows, :])
+            values[k] = held.tile([P, S], F32, name=f"values{k}")
+            gates[k] = held.tile([P, S], F32, name=f"gates{k}")
+            nc.sync.dma_start(values[k][:], tab[0, rows, :])
             for j in range(PIECES):
                 if j == PIECES // 2:
-                    nc.sync.dma_start(gates[:], tab[1, rows, :])
-                nc.sync.dma_start(streams[j][:], y[rows, j * PIECE : (j + 1) * PIECE])
+                    nc.sync.dma_start(gates[k][:], tab[1, rows, :])
+                streams[k, j] = held.tile([P, PIECE], F32, name=f"stream{k}_{j}")
+                nc.sync.dma_start(streams[k, j][:], y[rows, j * PIECE : (j + 1) * PIECE])
 
-            for j in range(PIECES):
-                entries = offsets[:, j * PIECE // GROUP : (j + 1) * PIECE // GROUP]
-                scaled = held.tile([P, PIECE], F32, name=f"scaled{k}_{j}")
-                gated = held.tile([P, PIECE], F32, name=f"gated{k}_{j}")
-                x = held.tile([P, PIECE], BF16, name=f"x{k}_{j}")
-                nc.vector.tensor_tensor(scaled[:], values[:].indirect(entries), streams[j][:], MULT)
-                nc.scalar.activation(gated[:], gates[:].indirect(entries), SILU)
-                nc.vector.tensor_tensor(x[:], scaled[:], gated[:], MULT)
-                nc.tensor.matmul(banks[j][:], weights[:, k, :], x[:], start=k == 0, stop=k == BLOCKS - 1)
+        nc.sync.dma_start(weights[:], w.rearrange("(k p) m -> p k m", p=P))
+        nc.sync.dma_start(bias[:], b)
+
+        scaled, gated = {}, {}
+
+        def look_up(k, j):
+            entries = offsets[:, j * PIECE // GROUP : (j + 1) * PIECE // GROUP]
+            scaled[k, j] = held.tile([P, PIECE], F32, name=f"scaled{k}_{j}")
+            gated[k, j] = held.tile([P, PIECE], F32, name=f"gated{k}_{j}")
+            nc.vector.tensor_tensor(scaled[k, j][:], values[k][:].indirect(entries), streams[k, j][:], MULT)
+            nc.scalar.activation(gated[k, j][:], gates[k][:].indirect(entries), SILU)
+
+        def project(k, j):
+            width = PIECE // parts[j]
+            for h in range(parts[j]):
+                cols = slice(h * width, (h + 1) * width)
+                x = held.tile([P, width], BF16, name=f"x{k}_{j}_{h}")
+                nc.vector.tensor_tensor(x[:], scaled[k, j][:, cols], gated[k, j][:, cols], MULT)
+                nc.tensor.matmul(banks[j, h][:], weights[:, k, :], x[:], start=k == 0, stop=k == BLOCKS - 1)
+
+        units = [(k, j) for k in range(BLOCKS) for j in range(PIECES)]
+        for step in range(len(units) + LAG):
+            if step < len(units):
+                look_up(*units[step])
+            if step >= LAG:
+                project(*units[step - LAG])
 
         for j in range(PIECES):
-            result = held.tile([M, PIECE], F32, name=f"result{j}")
-            if j % 2 == 0:
-                nc.scalar.activation(result[:], banks[j][:], RELU, bias=bias[:])
-            else:
-                nc.vector.tensor_scalar(result[:], banks[j][:], bias[:], 0.0, ADD, MAX)
-            nc.sync.dma_start(out[:, j * PIECE : (j + 1) * PIECE], result[:])
+            width = PIECE // parts[j]
+            for h in range(parts[j]):
+                result = held.tile([M, width], F32, name=f"result{j}_{h}")
+                if h == 0:
+                    nc.scalar.activation(result[:], banks[j, h][:], RELU, bias=bias[:])
+                else:
+                    nc.vector.tensor_scalar(result[:], banks[j, h][:], bias[:], 0.0, ADD, MAX)
+                first = j * PIECE + h * width
+                nc.sync.dma_start(out[:, first : first + width], result[:])

@@ -7,6 +7,7 @@ SILU, RELU = mybir.ActivationFunctionType.Silu, mybir.ActivationFunctionType.Rel
 P = 128
 K, S, N, M = 256, 2048, 2048, 128
 PIECE = 512
+HALF = PIECE // 2
 GROUP = 16
 BLOCKS, PIECES = K // P, N // PIECE
 
@@ -24,11 +25,8 @@ def tile_lookup_vg_mulsilu_relu_kernel(tc, tab, y, w, b, offs, out):
         offsets = held.tile([P, N // GROUP], U16, name="offsets")
         weights = held.tile([P, BLOCKS, M], BF16, name="weights")
         bias = held.tile([M, 1], F32, name="bias")
-        parts = {j: 2 if j >= PIECES - LAG else 1 for j in range(PIECES)}
         banks = {
-            (j, h): psum.tile([M, PIECE // parts[j]], F32, name=f"bank{j}_{h}")
-            for j in range(PIECES)
-            for h in range(parts[j])
+            (j, h): psum.tile([M, HALF], F32, name=f"bank{j}_{h}") for j in range(PIECES) for h in range(2)
         }
 
         nc.sync.dma_start(offsets[:], offs)
@@ -43,12 +41,13 @@ def tile_lookup_vg_mulsilu_relu_kernel(tc, tab, y, w, b, offs, out):
             rows = slice(k * P, (k + 1) * P)
             values[k] = held.tile([P, S], F32, name=f"values{k}")
             gates[k] = held.tile([P, S], F32, name=f"gates{k}")
+            streams[k] = held.tile([P, N], F32, name=f"stream{k}")
             nc.sync.dma_start(values[k][:], tab[0, rows, :])
-            for j in range(PIECES):
-                if j == PIECES // 2:
-                    nc.sync.dma_start(gates[k][:], tab[1, rows, :])
-                streams[k, j] = held.tile([P, PIECE], F32, name=f"stream{k}_{j}")
-                nc.sync.dma_start(streams[k, j][:], y[rows, j * PIECE : (j + 1) * PIECE])
+            nc.sync.dma_start(streams[k][:, : LAG * PIECE], y[rows, : LAG * PIECE])
+            nc.sync.dma_start(gates[k][:], tab[1, rows, :])
+            for j in range(LAG, PIECES):
+                cols = slice(j * PIECE, (j + 1) * PIECE)
+                nc.sync.dma_start(streams[k][:, cols], y[rows, cols])
 
         nc.sync.dma_start(weights[:], w.rearrange("(k p) m -> p k m", p=P))
         nc.sync.dma_start(bias[:], b)
@@ -59,14 +58,13 @@ def tile_lookup_vg_mulsilu_relu_kernel(tc, tab, y, w, b, offs, out):
             entries = offsets[:, j * PIECE // GROUP : (j + 1) * PIECE // GROUP]
             scaled[k, j] = held.tile([P, PIECE], F32, name=f"scaled{k}_{j}")
             gated[k, j] = held.tile([P, PIECE], F32, name=f"gated{k}_{j}")
-            nc.vector.tensor_tensor(scaled[k, j][:], values[k][:].indirect(entries), streams[k, j][:], MULT)
+            nc.vector.tensor_tensor(scaled[k, j][:], values[k][:].indirect(entries), streams[k][:, j * PIECE : (j + 1) * PIECE], MULT)
             nc.scalar.activation(gated[k, j][:], gates[k][:].indirect(entries), SILU)
 
         def project(k, j):
-            width = PIECE // parts[j]
-            for h in range(parts[j]):
-                cols = slice(h * width, (h + 1) * width)
-                x = held.tile([P, width], BF16, name=f"x{k}_{j}_{h}")
+            for h in range(2):
+                cols = slice(h * HALF, (h + 1) * HALF)
+                x = held.tile([P, HALF], BF16, name=f"x{k}_{j}_{h}")
                 nc.vector.tensor_tensor(x[:], scaled[k, j][:, cols], gated[k, j][:, cols], MULT)
                 nc.tensor.matmul(banks[j, h][:], weights[:, k, :], x[:], start=k == 0, stop=k == BLOCKS - 1)
 
@@ -78,12 +76,11 @@ def tile_lookup_vg_mulsilu_relu_kernel(tc, tab, y, w, b, offs, out):
                 project(*units[step - LAG])
 
         for j in range(PIECES):
-            width = PIECE // parts[j]
-            for h in range(parts[j]):
-                result = held.tile([M, width], F32, name=f"result{j}_{h}")
-                if h == 0:
-                    nc.scalar.activation(result[:], banks[j, h][:], RELU, bias=bias[:])
-                else:
+            for h in range(2):
+                result = held.tile([M, HALF], F32, name=f"result{j}_{h}")
+                if h == 1 and j >= PIECES - LAG:
                     nc.vector.tensor_scalar(result[:], banks[j, h][:], bias[:], 0.0, ADD, MAX)
-                first = j * PIECE + h * width
-                nc.sync.dma_start(out[:, first : first + width], result[:])
+                else:
+                    nc.scalar.activation(result[:], banks[j, h][:], RELU, bias=bias[:])
+                first = j * PIECE + h * HALF
+                nc.sync.dma_start(out[:, first : first + HALF], result[:])

import concourse.mybir as mybir

F32, BF16, U16 = mybir.dt.float32, mybir.dt.bfloat16, mybir.dt.uint16
MULT, ADD, MAX = mybir.AluOpType.mult, mybir.AluOpType.add, mybir.AluOpType.max
SILU, RELU = mybir.ActivationFunctionType.Silu, mybir.ActivationFunctionType.Relu

P = 128
K, S, N, M = 256, 2048, 2048, 128
PIECE = 512
HALF = PIECE // 2
GROUP = 16
BLOCKS, PIECES = K // P, N // PIECE

LAG = PIECES // 2

FLOPS = 2 * K * M * N


def tile_lookup_vg_mulsilu_relu_kernel(tc, tab, y, w, b, offs, out):
    nc = tc.nc
    with (
        tc.tile_pool(name="held", bufs=1) as held,
        tc.psum_pool(name="psum", bufs=1) as psum,
    ):
        offsets = held.tile([P, N // GROUP], U16, name="offsets")
        weights = held.tile([P, BLOCKS, M], BF16, name="weights")
        bias = held.tile([M, 1], F32, name="bias")
        banks = {
            (j, h): psum.tile([M, HALF], F32, name=f"bank{j}_{h}") for j in range(PIECES) for h in range(2)
        }

        nc.sync.dma_start(offsets[:], offs)

        scratch = held.tile([P, 1], F32, name="scratch")
        warmed = held.tile([P, 1], F32, name="warmed")
        nc.vector.memset(scratch[:], 0.0)
        nc.scalar.activation(warmed[:], scratch[:], SILU)

        values, gates, streams = {}, {}, {}
        for k in range(BLOCKS):
            rows = slice(k * P, (k + 1) * P)
            values[k] = held.tile([P, S], F32, name=f"values{k}")
            gates[k] = held.tile([P, S], F32, name=f"gates{k}")
            streams[k] = held.tile([P, N], F32, name=f"stream{k}")
            nc.sync.dma_start(values[k][:], tab[0, rows, :])
            nc.sync.dma_start(streams[k][:, : LAG * PIECE], y[rows, : LAG * PIECE])
            nc.sync.dma_start(gates[k][:], tab[1, rows, :])
            for j in range(LAG, PIECES):
                cols = slice(j * PIECE, (j + 1) * PIECE)
                nc.sync.dma_start(streams[k][:, cols], y[rows, cols])

        nc.sync.dma_start(weights[:], w.rearrange("(k p) m -> p k m", p=P))
        nc.sync.dma_start(bias[:], b)

        scaled, gated = {}, {}

        def look_up(k, j):
            entries = offsets[:, j * PIECE // GROUP : (j + 1) * PIECE // GROUP]
            scaled[k, j] = held.tile([P, PIECE], F32, name=f"scaled{k}_{j}")
            gated[k, j] = held.tile([P, PIECE], F32, name=f"gated{k}_{j}")
            nc.vector.tensor_tensor(scaled[k, j][:], values[k][:].indirect(entries), streams[k][:, j * PIECE : (j + 1) * PIECE], MULT)
            nc.scalar.activation(gated[k, j][:], gates[k][:].indirect(entries), SILU)

        def project(k, j):
            for h in range(2):
                cols = slice(h * HALF, (h + 1) * HALF)
                x = held.tile([P, HALF], BF16, name=f"x{k}_{j}_{h}")
                nc.vector.tensor_tensor(x[:], scaled[k, j][:, cols], gated[k, j][:, cols], MULT)
                nc.tensor.matmul(banks[j, h][:], weights[:, k, :], x[:], start=k == 0, stop=k == BLOCKS - 1)

        units = [(k, j) for k in range(BLOCKS) for j in range(PIECES)]
        for step in range(len(units) + LAG):
            if step < len(units):
                look_up(*units[step])
            if step >= LAG:
                project(*units[step - LAG])

        for j in range(PIECES):
            for h in range(2):
                result = held.tile([M, HALF], F32, name=f"result{j}_{h}")
                if h == 1 and j >= PIECES - LAG:
                    nc.vector.tensor_scalar(result[:], banks[j, h][:], bias[:], 0.0, ADD, MAX)
                else:
                    nc.scalar.activation(result[:], banks[j, h][:], RELU, bias=bias[:])
                first = j * PIECE + h * HALF
                nc.sync.dma_start(out[:, first : first + HALF], result[:])
